import numpy as np
import ml_dtypes


def mxq(x, axis, fmt="e4m3"):
    dtype, down = {"e4m3": (ml_dtypes.float8_e4m3fn, 7), "e5m2": (ml_dtypes.float8_e5m2, 14)}[fmt]
    v = np.moveaxis(np.asarray(x, np.float32).astype(ml_dtypes.bfloat16).astype(np.float64), axis, -1)
    blocks = v.reshape(v.shape[:-1] + (-1, 32))
    amax = np.abs(blocks).max(-1, keepdims=True)
    byte = np.maximum(np.where(amax > 0, np.frexp(amax)[1] - 1 + 127, 0) - down, 1)
    scale = np.exp2(byte - 127.0)
    codes = (blocks / scale).astype(np.float32).astype(dtype).astype(np.float64)
    return np.moveaxis((codes * scale).reshape(v.shape), -1, axis)


WIDE = False


def mx_kscale(k):
    if not WIDE:
        return np.ones(k)
    levels = np.array([10, -10, 5, -5, 0])
    if k % 512:
        return np.exp2(np.random.permutation(np.resize(levels, k // 32))).repeat(32)
    a = np.empty((k // 512, 16))
    for p in range(k // 512):
        a[p, :8] = np.random.permutation(np.resize(levels, 8))
        for g in range(8):
            far = levels[np.abs(levels - a[p, g]) >= 10]
            a[p, g + 8] = far[np.random.randint(len(far))]
    return np.exp2(a.ravel()).repeat(32)


def f64(x):
    return np.asarray(x).astype(np.float64)


def striped(idx):
    return np.tile(idx.reshape(-1, 16).T, (8, 1)).astype(np.uint16)


def unstriped(offs):
    return offs[:16].T.reshape(-1).astype(np.int64)


def relu(v):
    return np.maximum(v, 0.0)


K, T, E, C, H, N = 512, 768, 12, 128, 512, 256


def by_expert(wq, xq):
    return np.concatenate([wq[e].T @ xq[:, e * C:(e + 1) * C] for e in range(E)], axis=1)


def setup_inputs():
    n = np.random.standard_normal
    s = mx_kscale(K)[:, None]
    u = mx_kscale(H)
    first = np.random.permutation(np.repeat(np.arange(E), T // E))
    second = (first + 1 + np.random.permutation(np.repeat(np.arange(E - 1), -(-T // (E - 1)))[:T])) % E
    while np.bincount(second, minlength=E).max() != T // E:
        load = np.bincount(second, minlength=E); hi, lo = int(load.argmax()), int(load.argmin())
        t = np.flatnonzero((second == hi) & (first != lo))[0]; second[t] = lo
    slot_token = np.empty(E * C, np.int64); pos = np.empty((2, T), np.int64); fill = np.zeros(E, np.int64)
    place = np.stack([np.random.permutation(C) for _ in range(E)])
    for r, deal in enumerate((first, second)):
        for t in np.random.permutation(T):
            e = deal[t]; j = e * C + place[e, fill[e]]; fill[e] += 1; slot_token[j] = t; pos[r, t] = j
    g = np.random.uniform(0.2, 0.8, T)
    return {
        "xT": (n((K, T)) * s).astype(np.float32),
        "w1": (n((E + 1, K, H)) / np.sqrt(K) / s[None] * u[None, None, :]).astype(np.float32),
        "w2": (n((E + 1, H, N)) / np.sqrt(H) / u[None, :, None]).astype(np.float32),
        "gate": np.stack([np.tile(g, (N, 1)), np.tile(1.0 - g, (N, 1))]).astype(np.float32),
        "offs": striped(slot_token),
        "pos1": striped(pos[0]),
        "pos2": striped(pos[1]),
    }


def reference(xT, w1, w2, gate, offs, pos1, pos2):
    idx = unstriped(offs)
    w1q, w2q = mxq(f64(w1), 1, "e4m3"), mxq(f64(w2), 1, "e4m3")
    xs = mxq(f64(xT), 0, "e4m3")
    hs = relu(w1q[E].T @ xs)
    ys = w2q[E].T @ mxq(hs, 0, "e4m3")
    xq = mxq(f64(xT)[:, idx], 0, "e4m3")
    h = relu(by_expert(w1q, xq))
    y = by_expert(w2q, mxq(h, 0, "e4m3"))
    return ys + f64(gate[0]) * y[:, unstriped(pos1)] + f64(gate[1]) * y[:, unstriped(pos2)]

@@ -1,0 +1,284 @@
+from contextlib import ExitStack
+
+import concourse.mybir as mybir
+
+K, T, E, C, H, N = 512, 768, 12, 128, 512, 256
+S = E * C
+P = 128
+J = 4
+R = N // P
+FLOPS = 2 * (S + T) * (K * H + H * N)
+
+F32 = mybir.dt.float32
+BF16 = mybir.dt.bfloat16
+U32 = mybir.dt.uint32
+U16 = mybir.dt.uint16
+U8 = mybir.dt.uint8
+FP8X4 = mybir.dt.float8_e4m3fn_x4
+RELU = mybir.ActivationFunctionType.Relu
+MULT = mybir.AluOpType.mult
+ADD = mybir.AluOpType.add
+
+CHUNK = 512
+W1S = (1, 3, 5, 7, 9)
+VW2 = 0
+VW2S = 64
+AHEAD = 5
+W1S_PARTS = 4
+
+
+def tile_moe_shr_mlp_relu_kernel(tc, xT, w1, w2, gate, offs, pos1, pos2, out):
+    nc = tc.nc
+    with ExitStack() as ctx:
+        lists = ctx.enter_context(tc.tile_pool(name="lists", bufs=1))
+        keep = ctx.enter_context(tc.tile_pool(name="keep", bufs=1))
+        raw = ctx.enter_context(tc.tile_pool(name="raw", bufs=6))
+        grp = ctx.enter_context(tc.tile_pool(name="grp", bufs=3))
+        cod = ctx.enter_context(tc.tile_pool(name="cod", bufs=3))
+        hid = ctx.enter_context(tc.tile_pool(name="hid", bufs=3))
+        fin = ctx.enter_context(tc.tile_pool(name="fin", bufs=2))
+        pa = ctx.enter_context(tc.psum_pool(name="pa", bufs=3))
+        py = ctx.enter_context(tc.psum_pool(name="py", bufs=2))
+        ps = ctx.enter_context(tc.psum_pool(name="ps", bufs=1))
+
+        offs_sb = lists.tile([P, S // 16], U16, name="offs_sb")
+        pos1_sb = lists.tile([P, T // 16], U16, name="pos1_sb")
+        pos2_sb = lists.tile([P, T // 16], U16, name="pos2_sb")
+
+        nc.sync.dma_start(offs_sb[:], offs)
+        x_raw = keep.tile([P, J, T], F32, name="x_raw")
+        x_rows = xT.rearrange("(p j) t -> p j t", j=J)
+        for u in range(2):
+            nc.sync.dma_start(out=x_raw[:, 2 * u : 2 * u + 2, :], in_=x_rows[:, 2 * u : 2 * u + 2, :])
+
+        w1_raw, w2_raw = {}, {}
+
+        def load_w1(e):
+            w1_raw[e] = raw.tile([P, J, H], F32, name="w1_raw")
+            nc.sync.dma_start(out=w1_raw[e][:], in_=w1[e].rearrange("(p j) i -> p j i", j=J))
+
+        def load_w2(e):
+            w2_raw[e] = raw.tile([P, J, N], F32, name="w2_raw")
+            nc.sync.dma_start(out=w2_raw[e][:], in_=w2[e].rearrange("(p j) n -> p j n", j=J))
+
+        gates = {}
+
+        def load_gate(r):
+            for c in range(2):
+                gates[c, r] = keep.tile([P, T], F32, name=f"gate{c}{r}")
+                nc.sync.dma_start(out=gates[c, r][:], in_=gate[c, r * P : (r + 1) * P, :])
+
+        def load_step(s):
+            if s <= E:
+                if s == E:
+                    load_w2(E - 1)
+                    nc.sync.dma_start(pos1_sb[:], pos1)
+                    nc.sync.dma_start(pos2_sb[:], pos2)
+                    load_gate(0)
+                load_w1(s)
+                if 0 < s < E:
+                    load_w2(s - 1)
+                if s == E:
+                    load_w2(E)
+                    load_gate(1)
+
+        x_pair = keep.tile([P, 2 * T * 2], BF16, name="x_pair", align_bytes=64)
+
+        def cast_pair(u):
+            dst = x_pair[:, u * 2 * T : (u + 1) * 2 * T].rearrange("p (b i e) -> p b e i", i=4, e=2)
+            src = x_raw[:, 2 * u : 2 * u + 2, :].rearrange("p e (b i) -> p b e i", i=4)
+            if u == 0:
+                nc.vector.tensor_copy(out=dst, in_=src)
+            else:
+                nc.scalar.copy(out=dst, in_=src)
+
+        xg = {}
+        xc = {}
+
+        def gather(c):
+            xg[c] = grp.tile([P, CHUNK * J], BF16, name="xg", align_bytes=64)
+            words = xg[c][:].bitcast(U32).rearrange("p (s u) -> p s u", u=2)
+            for u in range(2):
+                window = x_pair[:, u * 2 * T : (u + 1) * 2 * T].bitcast(U32)
+                lst = offs_sb[:, c * (CHUNK // 16) : (c + 1) * (CHUNK // 16)]
+                nc.vector.tensor_copy(out=words[:, :, u], in_=window.indirect(lst))
+
+        def quant(src, width, cname, pool):
+            codes = pool.tile([P, width], U32, name=cname, align_bytes=64)
+            scales = pool.tile([P, width], U8, name=cname + "_sc", align_bytes=64)
+            nc.vector.quantize_mx(out=codes[:].bitcast(FP8X4), scales=scales[:], in_=src)
+            return codes, scales
+
+        def quant_x(c):
+            xc[c] = quant(xg[c][:], CHUNK, "xq", cod)
+
+        w1_grp, w2_grp, w1_q, w2_q = {}, {}, {}, {}
+
+        def group_w1(e, on_scalar, parts=1):
+            w1_grp[e] = grp.tile([P, H * J], BF16, name="w1_grp", align_bytes=64)
+            dst = w1_grp[e][:].rearrange("p (t m j) -> p m j t", t=4, j=J)
+            src = w1_raw[e][:].rearrange("p j (m t) -> p m j t", t=4)
+            copy = nc.scalar.copy if on_scalar else nc.vector.tensor_copy
+            step = P // parts
+            for m in range(0, P, step):
+                copy(out=dst[:, m : m + step], in_=src[:, m : m + step])
+
+        def group_w2(e, on_vector):
+            w2_grp[e] = grp.tile([P, N * J], BF16, name="w2_grp", align_bytes=64)
+            dst = w2_grp[e][:].rearrange("p (b i j) -> p b j i", i=4, j=J)
+            src = w2_raw[e][:].rearrange("p j (b i) -> p b j i", i=4)
+            v = on_vector
+            if v > 0:
+                nc.vector.tensor_copy(out=dst[:, :v], in_=src[:, :v])
+            if v < N // 4:
+                nc.scalar.copy(out=dst[:, v:], in_=src[:, v:])
+
+        def quant_w1(e):
+            w1_q[e] = quant(w1_grp[e][:], H, "w1_q", cod)
+
+        def quant_w2(e):
+            w2_q[e] = quant(w2_grp[e][:], N, "w2_q", cod)
+
+        y_slots = [keep.tile([P, S], F32, name=f"y{r}") for r in range(R)]
+        h4, hq = {}, {}
+
+        def layer1(key, wq, x_codes, x_scales, cols, h_dst):
+            a = pa.tile([P, J, C], F32, name="a")
+            for t in range(J):
+                nc.tensor.matmul_mx(
+                    out=a[:, t, :],
+                    lhsT=wq[0][:, t * P : (t + 1) * P].bitcast(FP8X4),
+                    lhsT_scale=wq[1][:, t * P : (t + 1) * P],
+                    rhs=x_codes[:, cols].bitcast(FP8X4),
+                    rhs_scale=x_scales[:, cols],
+                    start=True,
+                    stop=True,
+                )
+            nc.scalar.activation(
+                out=h_dst.rearrange("p (c t) -> p c t", t=J),
+                in_=a[:].rearrange("p t c -> p c t"),
+                func=RELU,
+            )
+
+        def layer1_routed(e):
+            h4[e] = hid.tile([P, C * J], BF16, name="h4", align_bytes=64)
+            c, o = divmod(e * C, CHUNK)
+            layer1(e, w1_q[e], xc[c][0], xc[c][1], slice(o, o + C), h4[e][:])
+
+        def quant_h(e):
+            hq[e] = quant(h4[e][:], C, "hq", hid)
+
+        y_ps = {}
+
+        def layer2_routed(e):
+            if e % 2 == 0:
+                y_ps[0] = py.tile([P, R, 2, C], F32, name="y_ps")
+            y = y_ps[0]
+            for r in range(R):
+                nc.tensor.matmul_mx(
+                    out=y[:, r, e % 2, :],
+                    lhsT=w2_q[e][0][:, r * P : (r + 1) * P].bitcast(FP8X4),
+                    lhsT_scale=w2_q[e][1][:, r * P : (r + 1) * P],
+                    rhs=hq[e][0][:].bitcast(FP8X4),
+                    rhs_scale=hq[e][1][:],
+                    start=True,
+                    stop=True,
+                )
+            if e % 2 == 1:
+                for r in range(R):
+                    nc.scalar.copy(
+                        out=y_slots[r][:, (e - 1) * C : (e + 1) * C],
+                        in_=y[:, r, :, :].rearrange("p e c -> p (e c)"),
+                    )
+
+        for s in range(AHEAD):
+            load_step(s)
+        cast_pair(0)
+        cast_pair(1)
+        gather(0)
+        x4 = keep.tile([P, T * J], BF16, name="x4", align_bytes=64)
+        nc.gpsimd.tensor_scalar(
+            out=x4[:].rearrange("p (b i j) -> p b j i", i=4, j=J),
+            in0=x_raw[:].rearrange("p j (b i) -> p b j i", i=4),
+            scalar1=1.0,
+            scalar2=0.0,
+            op0=MULT,
+            op1=ADD,
+        )
+        for s in range(E + 4):
+            load_step(s + AHEAD)
+            if s == 0:
+                quant_x(0)
+            if s in (2, 6):
+                gather(1 if s == 2 else 2)
+            if s in (3, 7):
+                quant_x(1 if s == 3 else 2)
+            if s < E:
+                group_w1(s, s in W1S)
+            if 1 <= s <= E:
+                group_w2(s - 1, 32 if s == E else VW2S if s - 1 in W1S else VW2)
+                quant_w1(s - 1)
+            if 2 <= s <= E + 1:
+                quant_w2(s - 2)
+                layer1_routed(s - 2)
+            if s == 4:
+                xs_a = quant(x4[:, : CHUNK * J], CHUNK, "xs_a", keep)
+                xs_b = quant(x4[:, CHUNK * J :], T - CHUNK, "xs_b", keep)
+            if 3 <= s <= E + 2:
+                quant_h(s - 3)
+            if 3 <= s <= E + 2:
+                layer2_routed(s - 3)
+
+        g = {}
+
+        def pick(c, r):
+            g[c, r] = fin.tile([P, T], F32, name=f"g{c}")
+            lst = pos1_sb if c == 0 else pos2_sb
+            nc.vector.tensor_tensor(out=g[c, r][:], in0=y_slots[r][:].indirect(lst[:]), in1=gates[c, r][:], op=MULT)
+
+        both = {}
+
+        def add_both(r):
+            both[r] = fin.tile([P, T], F32, name="both")
+            nc.vector.tensor_tensor(out=both[r][:], in0=g[0, r][:], in1=g[1, r][:], op=ADD)
+
+        group_w1(E, True, W1S_PARTS)
+        group_w2(E, 0)
+        pick(0, 0)
+        pick(1, 0)
+        quant_w1(E)
+        hs4 = keep.tile([P, T * J], BF16, name="hs4", align_bytes=64)
+        for c in range(T // C):
+            xs, o = (xs_a, c * C) if c * C < CHUNK else (xs_b, c * C - CHUNK)
+            layer1("s", w1_q[E], xs[0], xs[1], slice(o, o + C), hs4[:, c * C * J : (c + 1) * C * J])
+        pick(0, 1)
+        quant_w2(E)
+        pick(1, 1)
+        add_both(0)
+        add_both(1)
+        hs_a = quant(hs4[:, : CHUNK * J], CHUNK, "hs_a", keep)
+        hs_b = quant(hs4[:, CHUNK * J :], T - CHUNK, "hs_b", keep)
+
+        bank0 = ps.tile([P, CHUNK], F32, name="bank0")
+        bank1 = ps.tile([P, 2, T - CHUNK], F32, name="bank1")
+        bank2 = ps.tile([P, CHUNK], F32, name="bank2")
+        pieces = [
+            (0, slice(0, CHUNK), bank0[:], hs_a),
+            (1, slice(0, CHUNK), bank2[:], hs_a),
+            (0, slice(CHUNK, T), bank1[:, 0, :], hs_b),
+            (1, slice(CHUNK, T), bank1[:, 1, :], hs_b),
+        ]
+        for r, cols, dst, hsq in pieces:
+            nc.tensor.matmul_mx(
+                out=dst,
+                lhsT=w2_q[E][0][:, r * P : (r + 1) * P].bitcast(FP8X4),
+                lhsT_scale=w2_q[E][1][:, r * P : (r + 1) * P],
+                rhs=hsq[0][:].bitcast(FP8X4),
+                rhs_scale=hsq[1][:],
+                start=True,
+                stop=True,
+            )
+        for r, cols, src, hsq in pieces:
+            res = fin.tile([P, cols.stop - cols.start], F32, name=f"res{r}{cols.start}")
+            nc.vector.tensor_tensor(out=res[:], in0=src, in1=both[r][:, cols], op=ADD)
+            nc.sync.dma_start(out=out[r * P : (r + 1) * P, cols], in_=res[:])

@@ -20,11 +20,35 @@ MULT = mybir.AluOpType.mult
 ADD = mybir.AluOpType.add
 
 CHUNK = 512
-W1S = (1, 3, 5, 7, 9)
+W1S = (3, 7)
 VW2 = 0
 VW2S = 64
-AHEAD = 5
-W1S_PARTS = 4
+VW2L = 32
+AHEAD = 4
+W1_PARTS = 1
+VM = 96
+RAW1 = 5
+RAW2 = 4
+GRP = 2
+XP1 = 'S'
+X4E = 'S'
+SPOS = 12
+LAG_Q1 = 1
+LAG_W2 = 1
+LAG_Q2 = 2
+LAG_L1 = 2
+LAG_QH = 3
+LAG_L2 = 3
+ORDER = ('w1', 'q1', 'l1', 'w2', 'q2', 'qh', 'l2')
+G0_STEP = 1
+G1_STEP = 2
+G2_STEP = 7
+X4_STEP = 1
+XSQ_STEP = 3
+PA = 3
+RELUV = (11,)
+YV = ((11, 0),)
+HALVES = 3
 
 
 def tile_moe_shr_mlp_relu_kernel(tc, xT, w1, w2, gate, offs, pos1, pos2, out):
@@ -32,19 +56,23 @@ def tile_moe_shr_mlp_relu_kernel(tc, xT, w1, w2, gate, offs, pos1, pos2, out):
     with ExitStack() as ctx:
         lists = ctx.enter_context(tc.tile_pool(name="lists", bufs=1))
         keep = ctx.enter_context(tc.tile_pool(name="keep", bufs=1))
-        raw = ctx.enter_context(tc.tile_pool(name="raw", bufs=6))
-        grp = ctx.enter_context(tc.tile_pool(name="grp", bufs=3))
+        raw1 = ctx.enter_context(tc.tile_pool(name="raw1", bufs=RAW1))
+        raw2 = ctx.enter_context(tc.tile_pool(name="raw2", bufs=RAW2))
+        grp = ctx.enter_context(tc.tile_pool(name="grp", bufs=GRP))
         cod = ctx.enter_context(tc.tile_pool(name="cod", bufs=3))
         hid = ctx.enter_context(tc.tile_pool(name="hid", bufs=3))
         fin = ctx.enter_context(tc.tile_pool(name="fin", bufs=2))
-        pa = ctx.enter_context(tc.psum_pool(name="pa", bufs=3))
+        pa = ctx.enter_context(tc.psum_pool(name="pa", bufs=PA))
         py = ctx.enter_context(tc.psum_pool(name="py", bufs=2))
         ps = ctx.enter_context(tc.psum_pool(name="ps", bufs=1))
+
+        seq = list(range(E))
+        seq.insert(SPOS, E)
+        NE = E + 1
 
         offs_sb = lists.tile([P, S // 16], U16, name="offs_sb")
         pos1_sb = lists.tile([P, T // 16], U16, name="pos1_sb")
         pos2_sb = lists.tile([P, T // 16], U16, name="pos2_sb")
-
         nc.sync.dma_start(offs_sb[:], offs)
         x_raw = keep.tile([P, J, T], F32, name="x_raw")
         x_rows = xT.rearrange("(p j) t -> p j t", j=J)
@@ -54,40 +82,36 @@ def tile_moe_shr_mlp_relu_kernel(tc, xT, w1, w2, gate, offs, pos1, pos2, out):
         w1_raw, w2_raw = {}, {}
 
         def load_w1(e):
-            w1_raw[e] = raw.tile([P, J, H], F32, name="w1_raw")
+            w1_raw[e] = raw1.tile([P, J, H], F32, name="w1_raw")
             nc.sync.dma_start(out=w1_raw[e][:], in_=w1[e].rearrange("(p j) i -> p j i", j=J))
 
         def load_w2(e):
-            w2_raw[e] = raw.tile([P, J, N], F32, name="w2_raw")
+            w2_raw[e] = raw2.tile([P, J, N], F32, name="w2_raw")
             nc.sync.dma_start(out=w2_raw[e][:], in_=w2[e].rearrange("(p j) n -> p j n", j=J))
 
         gates = {}
 
         def load_gate(r):
-            for c in range(2):
-                gates[c, r] = keep.tile([P, T], F32, name=f"gate{c}{r}")
-                nc.sync.dma_start(out=gates[c, r][:], in_=gate[c, r * P : (r + 1) * P, :])
+            gates[r] = raw1.tile([P, 2, T], F32, name="w1_raw")
+            nc.sync.dma_start(out=gates[r][:], in_=gate[:, r * P : (r + 1) * P, :].rearrange("c p t -> p c t"))
 
         def load_step(s):
-            if s <= E:
-                if s == E:
-                    load_w2(E - 1)
-                    nc.sync.dma_start(pos1_sb[:], pos1)
-                    nc.sync.dma_start(pos2_sb[:], pos2)
-                    load_gate(0)
-                load_w1(s)
-                if 0 < s < E:
-                    load_w2(s - 1)
-                if s == E:
-                    load_w2(E)
-                    load_gate(1)
+            if s < NE:
+                load_w1(seq[s])
+            if 1 <= s <= NE:
+                load_w2(seq[s - 1])
+            if s == NE:
+                nc.sync.dma_start(pos1_sb[:], pos1)
+                nc.sync.dma_start(pos2_sb[:], pos2)
+                load_gate(0)
+                load_gate(1)
 
         x_pair = keep.tile([P, 2 * T * 2], BF16, name="x_pair", align_bytes=64)
 
         def cast_pair(u):
             dst = x_pair[:, u * 2 * T : (u + 1) * 2 * T].rearrange("p (b i e) -> p b e i", i=4, e=2)
             src = x_raw[:, 2 * u : 2 * u + 2, :].rearrange("p e (b i) -> p b e i", i=4)
-            if u == 0:
+            if u == 0 or XP1 == "V":
                 nc.vector.tensor_copy(out=dst, in_=src)
             else:
                 nc.scalar.copy(out=dst, in_=src)
@@ -112,22 +136,46 @@ def tile_moe_shr_mlp_relu_kernel(tc, xT, w1, w2, gate, offs, pos1, pos2, out):
         def quant_x(c):
             xc[c] = quant(xg[c][:], CHUNK, "xq", cod)
 
+        x4 = keep.tile([P, T * J], BF16, name="x4", align_bytes=64)
+
+        def cast_x4():
+            if X4E == "G":
+                nc.gpsimd.tensor_scalar(
+                    out=x4[:].rearrange("p (t j) -> p t j", j=J),
+                    in0=x_raw[:].rearrange("p j t -> p t j"),
+                    scalar1=1.0,
+                    scalar2=0.0,
+                    op0=MULT,
+                    op1=ADD,
+                )
+                return
+            dst = x4[:].rearrange("p (b i j) -> p b j i", i=4, j=J)
+            src = x_raw[:].rearrange("p j (b i) -> p b j i", i=4)
+            for lo, hi in ((0, CHUNK // 4), (CHUNK // 4, T // 4)):
+                if X4E == "S":
+                    nc.scalar.copy(out=dst[:, lo:hi], in_=src[:, lo:hi])
+                else:
+                    nc.vector.tensor_copy(out=dst[:, lo:hi], in_=src[:, lo:hi])
+
         w1_grp, w2_grp, w1_q, w2_q = {}, {}, {}, {}
 
-        def group_w1(e, on_scalar, parts=1):
+        def group_w1(e):
             w1_grp[e] = grp.tile([P, H * J], BF16, name="w1_grp", align_bytes=64)
             dst = w1_grp[e][:].rearrange("p (t m j) -> p m j t", t=4, j=J)
             src = w1_raw[e][:].rearrange("p j (m t) -> p m j t", t=4)
-            copy = nc.scalar.copy if on_scalar else nc.vector.tensor_copy
-            step = P // parts
-            for m in range(0, P, step):
-                copy(out=dst[:, m : m + step], in_=src[:, m : m + step])
+            vm = 0 if e in W1S else VM
+            if vm > 0:
+                nc.vector.tensor_copy(out=dst[:, :vm], in_=src[:, :vm])
+            if vm < P:
+                step = (P - vm) // (W1_PARTS if vm == 0 else 1)
+                for m in range(vm, P, step):
+                    nc.scalar.copy(out=dst[:, m : m + step], in_=src[:, m : m + step])
 
-        def group_w2(e, on_vector):
+        def group_w2(e):
             w2_grp[e] = grp.tile([P, N * J], BF16, name="w2_grp", align_bytes=64)
             dst = w2_grp[e][:].rearrange("p (b i j) -> p b j i", i=4, j=J)
             src = w2_raw[e][:].rearrange("p j (b i) -> p b j i", i=4)
-            v = on_vector
+            v = VW2L if e == E - 1 else VW2S if e in W1S else VW2
             if v > 0:
                 nc.vector.tensor_copy(out=dst[:, :v], in_=src[:, :v])
             if v < N // 4:
@@ -141,144 +189,134 @@ def tile_moe_shr_mlp_relu_kernel(tc, xT, w1, w2, gate, offs, pos1, pos2, out):
 
         y_slots = [keep.tile([P, S], F32, name=f"y{r}") for r in range(R)]
         h4, hq = {}, {}
+        hs4 = keep.tile([P, T * J], BF16, name="hs4", align_bytes=64)
+        xs, hs = {}, {}
 
-        def layer1(key, wq, x_codes, x_scales, cols, h_dst):
-            a = pa.tile([P, J, C], F32, name="a")
-            for t in range(J):
-                nc.tensor.matmul_mx(
-                    out=a[:, t, :],
-                    lhsT=wq[0][:, t * P : (t + 1) * P].bitcast(FP8X4),
-                    lhsT_scale=wq[1][:, t * P : (t + 1) * P],
-                    rhs=x_codes[:, cols].bitcast(FP8X4),
-                    rhs_scale=x_scales[:, cols],
-                    start=True,
-                    stop=True,
-                )
-            nc.scalar.activation(
-                out=h_dst.rearrange("p (c t) -> p c t", t=J),
-                in_=a[:].rearrange("p t c -> p c t"),
-                func=RELU,
+        def mx(dst, w, lo, xcodes, xscales):
+            nc.tensor.matmul_mx(
+                out=dst,
+                lhsT=w[0][:, lo : lo + P].bitcast(FP8X4),
+                lhsT_scale=w[1][:, lo : lo + P],
+                rhs=xcodes.bitcast(FP8X4),
+                rhs_scale=xscales,
+                start=True,
+                stop=True,
             )
 
-        def layer1_routed(e):
-            h4[e] = hid.tile([P, C * J], BF16, name="h4", align_bytes=64)
-            c, o = divmod(e * C, CHUNK)
-            layer1(e, w1_q[e], xc[c][0], xc[c][1], slice(o, o + C), h4[e][:])
+        def layer1(wq, x, cols, h_dst, on_vector):
+            a = pa.tile([P, J, C], F32, name="a")
+            for t in range(J):
+                mx(a[:, t, :], wq, t * P, x[0][:, cols], x[1][:, cols])
+            dst = h_dst.rearrange("p (c t) -> p c t", t=J)
+            src = a[:].rearrange("p t c -> p c t")
+            if on_vector:
+                nc.vector.tensor_scalar_max(dst, src, 0.0)
+            else:
+                nc.scalar.activation(out=dst, in_=src, func=RELU)
 
-        def quant_h(e):
-            hq[e] = quant(h4[e][:], C, "hq", hid)
+        def quant_xs():
+            xs["a"] = quant(x4[:, : CHUNK * J], CHUNK, "xs_a", keep)
+            xs["b"] = quant(x4[:, CHUNK * J :], T - CHUNK, "xs_b", keep)
+
+        def op_l1(e):
+            if e < E:
+                h4[e] = hid.tile([P, C * J], BF16, name="h4", align_bytes=64)
+                c, o = divmod(e * C, CHUNK)
+                layer1(w1_q[e], xc[c], slice(o, o + C), h4[e][:], e in RELUV)
+                return
+            for c in range(T // C):
+                x, o = (xs["a"], c * C) if c * C < CHUNK else (xs["b"], c * C - CHUNK)
+                layer1(w1_q[E], x, slice(o, o + C), hs4[:, c * C * J : (c + 1) * C * J], False)
+
+        def op_qh(e):
+            if e < E:
+                hq[e] = quant(h4[e][:], C, "hq", hid)
+                return
+            hs["a"] = quant(hs4[:, : CHUNK * J], CHUNK, "hs_a", keep)
+            hs["b"] = quant(hs4[:, CHUNK * J :], T - CHUNK, "hs_b", keep)
 
         y_ps = {}
+        bank0 = ps.tile([P, CHUNK], F32, name="bank0")
+        bank1 = ps.tile([P, 2, T - CHUNK], F32, name="bank1")
+        bank2 = ps.tile([P, CHUNK], F32, name="bank2")
+        ys = [
+            {"a": bank0[:], "b": bank1[:, 0, :]},
+            {"a": bank2[:], "b": bank1[:, 1, :]},
+        ]
 
-        def layer2_routed(e):
+        def op_l2(e):
+            if e == E:
+                for k in "ab":
+                    for r in range(R):
+                        mx(ys[r][k], w2_q[E], r * P, hs[k][0][:], hs[k][1][:])
+                return
             if e % 2 == 0:
                 y_ps[0] = py.tile([P, R, 2, C], F32, name="y_ps")
             y = y_ps[0]
             for r in range(R):
-                nc.tensor.matmul_mx(
-                    out=y[:, r, e % 2, :],
-                    lhsT=w2_q[e][0][:, r * P : (r + 1) * P].bitcast(FP8X4),
-                    lhsT_scale=w2_q[e][1][:, r * P : (r + 1) * P],
-                    rhs=hq[e][0][:].bitcast(FP8X4),
-                    rhs_scale=hq[e][1][:],
-                    start=True,
-                    stop=True,
-                )
+                mx(y[:, r, e % 2, :], w2_q[e], r * P, hq[e][0][:], hq[e][1][:])
             if e % 2 == 1:
                 for r in range(R):
-                    nc.scalar.copy(
-                        out=y_slots[r][:, (e - 1) * C : (e + 1) * C],
-                        in_=y[:, r, :, :].rearrange("p e c -> p (e c)"),
-                    )
+                    dst = y_slots[r][:, (e - 1) * C : (e + 1) * C]
+                    src = y[:, r, :, :].rearrange("p e c -> p (e c)")
+                    if (e, r) in YV:
+                        nc.vector.tensor_copy(out=dst, in_=src)
+                    else:
+                        nc.scalar.copy(out=dst, in_=src)
 
+        steps = {
+            "w1": (0, group_w1),
+            "w2": (LAG_W2, group_w2),
+            "q1": (LAG_Q1, quant_w1),
+            "q2": (LAG_Q2, quant_w2),
+            "l1": (LAG_L1, op_l1),
+            "qh": (LAG_QH, op_qh),
+            "l2": (LAG_L2, op_l2),
+        }
         for s in range(AHEAD):
             load_step(s)
         cast_pair(0)
         cast_pair(1)
-        gather(0)
-        x4 = keep.tile([P, T * J], BF16, name="x4", align_bytes=64)
-        nc.gpsimd.tensor_scalar(
-            out=x4[:].rearrange("p (b i j) -> p b j i", i=4, j=J),
-            in0=x_raw[:].rearrange("p j (b i) -> p b j i", i=4),
-            scalar1=1.0,
-            scalar2=0.0,
-            op0=MULT,
-            op1=ADD,
-        )
-        for s in range(E + 4):
+        if X4_STEP < 0:
+            cast_x4()
+        for s in range(NE + max(LAG_L2, LAG_QH) + 1):
             load_step(s + AHEAD)
-            if s == 0:
-                quant_x(0)
-            if s in (2, 6):
-                gather(1 if s == 2 else 2)
-            if s in (3, 7):
-                quant_x(1 if s == 3 else 2)
-            if s < E:
-                group_w1(s, s in W1S)
-            if 1 <= s <= E:
-                group_w2(s - 1, 32 if s == E else VW2S if s - 1 in W1S else VW2)
-                quant_w1(s - 1)
-            if 2 <= s <= E + 1:
-                quant_w2(s - 2)
-                layer1_routed(s - 2)
-            if s == 4:
-                xs_a = quant(x4[:, : CHUNK * J], CHUNK, "xs_a", keep)
-                xs_b = quant(x4[:, CHUNK * J :], T - CHUNK, "xs_b", keep)
-            if 3 <= s <= E + 2:
-                quant_h(s - 3)
-            if 3 <= s <= E + 2:
-                layer2_routed(s - 3)
+            if s == X4_STEP:
+                cast_x4()
+            if s == XSQ_STEP:
+                quant_xs()
+            for c, g in enumerate((G0_STEP, G1_STEP, G2_STEP)):
+                if s == g:
+                    gather(c)
+            for c, g in enumerate((G0_STEP, G1_STEP + 1, G2_STEP + 1)):
+                if s == g:
+                    quant_x(c)
+            for op in ORDER:
+                lag, fn = steps[op]
+                if 0 <= s - lag < NE:
+                    fn(seq[s - lag])
 
-        g = {}
-
-        def pick(c, r):
-            g[c, r] = fin.tile([P, T], F32, name=f"g{c}")
-            lst = pos1_sb if c == 0 else pos2_sb
-            nc.vector.tensor_tensor(out=g[c, r][:], in0=y_slots[r][:].indirect(lst[:]), in1=gates[c, r][:], op=MULT)
-
-        both = {}
-
-        def add_both(r):
-            both[r] = fin.tile([P, T], F32, name="both")
-            nc.vector.tensor_tensor(out=both[r][:], in0=g[0, r][:], in1=g[1, r][:], op=ADD)
-
-        group_w1(E, True, W1S_PARTS)
-        group_w2(E, 0)
-        pick(0, 0)
-        pick(1, 0)
-        quant_w1(E)
-        hs4 = keep.tile([P, T * J], BF16, name="hs4", align_bytes=64)
-        for c in range(T // C):
-            xs, o = (xs_a, c * C) if c * C < CHUNK else (xs_b, c * C - CHUNK)
-            layer1("s", w1_q[E], xs[0], xs[1], slice(o, o + C), hs4[:, c * C * J : (c + 1) * C * J])
-        pick(0, 1)
-        quant_w2(E)
-        pick(1, 1)
-        add_both(0)
-        add_both(1)
-        hs_a = quant(hs4[:, : CHUNK * J], CHUNK, "hs_a", keep)
-        hs_b = quant(hs4[:, CHUNK * J :], T - CHUNK, "hs_b", keep)
-
-        bank0 = ps.tile([P, CHUNK], F32, name="bank0")
-        bank1 = ps.tile([P, 2, T - CHUNK], F32, name="bank1")
-        bank2 = ps.tile([P, CHUNK], F32, name="bank2")
-        pieces = [
-            (0, slice(0, CHUNK), bank0[:], hs_a),
-            (1, slice(0, CHUNK), bank2[:], hs_a),
-            (0, slice(CHUNK, T), bank1[:, 0, :], hs_b),
-            (1, slice(CHUNK, T), bank1[:, 1, :], hs_b),
-        ]
-        for r, cols, dst, hsq in pieces:
-            nc.tensor.matmul_mx(
-                out=dst,
-                lhsT=w2_q[E][0][:, r * P : (r + 1) * P].bitcast(FP8X4),
-                lhsT_scale=w2_q[E][1][:, r * P : (r + 1) * P],
-                rhs=hsq[0][:].bitcast(FP8X4),
-                rhs_scale=hsq[1][:],
-                start=True,
-                stop=True,
-            )
-        for r, cols, src, hsq in pieces:
-            res = fin.tile([P, cols.stop - cols.start], F32, name=f"res{r}{cols.start}")
-            nc.vector.tensor_tensor(out=res[:], in0=src, in1=both[r][:, cols], op=ADD)
-            nc.sync.dma_start(out=out[r * P : (r + 1) * P, cols], in_=res[:])
+        w = T // HALVES
+        for r in range(R):
+            for h in range(HALVES if r == R - 1 else 1):
+                tok = slice(h * w, (h + 1) * w) if r == R - 1 else slice(0, T)
+                n = tok.stop - tok.start
+                g0 = fin.tile([P, T], F32, name="g0")
+                g1 = fin.tile([P, T], F32, name="g1")
+                both = fin.tile([P, T], F32, name="both")
+                for c, (g, lst) in enumerate(((g0, pos1_sb), (g1, pos2_sb))):
+                    nc.vector.tensor_tensor(
+                        out=g[:, :n],
+                        in0=y_slots[r][:].indirect(lst[:, tok.start // 16 : tok.stop // 16]),
+                        in1=gates[r][:, c, tok],
+                        op=MULT,
+                    )
+                nc.vector.tensor_tensor(out=both[:, :n], in0=g0[:, :n], in1=g1[:, :n], op=ADD)
+                for k, lo, hi in (("a", 0, CHUNK), ("b", CHUNK, T)):
+                    a, b = max(lo, tok.start), min(hi, tok.stop)
+                    if a < b:
+                        res = fin.tile([P, b - a], F32, name=f"res{r}{a}")
+                        nc.vector.tensor_tensor(
+                            out=res[:], in0=ys[r][k][:, a - lo : b - lo], in1=both[:, a - tok.start : b - tok.start], op=ADD
+                        )
+                        nc.sync.dma_start(out=out[r * P : (r + 1) * P, a:b], in_=res[:])

@@ -20,35 +20,38 @@ MULT = mybir.AluOpType.mult
 ADD = mybir.AluOpType.add
 
 CHUNK = 512
-W1S = (3, 7)
-VW2 = 0
-VW2S = 64
-VW2L = 32
-AHEAD = 4
-W1_PARTS = 1
-VM = 96
-RAW1 = 5
-RAW2 = 4
-GRP = 2
+GROUPS = ((0, 1), (2, 3), (4, 5), (6, 7), (8, 9), (10,), (11,))
+AHEAD = 3
+RAW1 = 4
+RAW2 = 3
+GRP1 = 2
+GRP2 = 2
+COD = 3
 XP1 = 'S'
-X4E = 'S'
-SPOS = 12
+X4E = 'G'
+SPOS = 0
+SHV = 0
+VMB = 64
+VMS = 80
+VWB = 0
+VWS = 64
 LAG_Q1 = 1
 LAG_W2 = 1
-LAG_Q2 = 2
-LAG_L1 = 2
-LAG_QH = 3
-LAG_L2 = 3
-ORDER = ('w1', 'q1', 'l1', 'w2', 'q2', 'qh', 'l2')
-G0_STEP = 1
-G1_STEP = 2
-G2_STEP = 7
-X4_STEP = 1
-XSQ_STEP = 3
+LAG_Q2 = 1
+LAG_L1 = 1
+LAG_QH = 2
+LAG_L2 = 2
+ORDER = ('q1', 'l1', 'w1', 'w2', 'qh', 'q2', 'l2')
+GCH = 512
+GL = 3
+GQ = 0
+X4_STEP = -1
+XSQ_STEP = 0
 PA = 3
-RELUV = (11,)
-YV = ((11, 0),)
-HALVES = 3
+RELUV = ()
+YV = ()
+HALVES = 1
+YSB = False
 
 
 def tile_moe_shr_mlp_relu_kernel(tc, xT, w1, w2, gate, offs, pos1, pos2, out):
@@ -58,17 +61,19 @@ def tile_moe_shr_mlp_relu_kernel(tc, xT, w1, w2, gate, offs, pos1, pos2, out):
         keep = ctx.enter_context(tc.tile_pool(name="keep", bufs=1))
         raw1 = ctx.enter_context(tc.tile_pool(name="raw1", bufs=RAW1))
         raw2 = ctx.enter_context(tc.tile_pool(name="raw2", bufs=RAW2))
-        grp = ctx.enter_context(tc.tile_pool(name="grp", bufs=GRP))
-        cod = ctx.enter_context(tc.tile_pool(name="cod", bufs=3))
-        hid = ctx.enter_context(tc.tile_pool(name="hid", bufs=3))
+        grp = ctx.enter_context(tc.tile_pool(name="grp", bufs=2))
+        grp1 = ctx.enter_context(tc.tile_pool(name="grp1", bufs=GRP1))
+        grp2 = ctx.enter_context(tc.tile_pool(name="grp2", bufs=GRP2))
+        cod = ctx.enter_context(tc.tile_pool(name="cod", bufs=COD))
+        hid = ctx.enter_context(tc.tile_pool(name="hid", bufs=2))
         fin = ctx.enter_context(tc.tile_pool(name="fin", bufs=2))
         pa = ctx.enter_context(tc.psum_pool(name="pa", bufs=PA))
         py = ctx.enter_context(tc.psum_pool(name="py", bufs=2))
         ps = ctx.enter_context(tc.psum_pool(name="ps", bufs=1))
 
-        seq = list(range(E))
-        seq.insert(SPOS, E)
-        NE = E + 1
+        seq = list(GROUPS)
+        seq.insert(SPOS, (E,))
+        NE = len(seq)
 
         offs_sb = lists.tile([P, S // 16], U16, name="offs_sb")
         pos1_sb = lists.tile([P, T // 16], U16, name="pos1_sb")
@@ -97,9 +102,10 @@ def tile_moe_shr_mlp_relu_kernel(tc, xT, w1, w2, gate, offs, pos1, pos2, out):
 
         def load_step(s):
             if s < NE:
-                load_w1(seq[s])
-            if 1 <= s <= NE:
-                load_w2(seq[s - 1])
+                for e in seq[s]:
+                    load_w1(e)
+                for e in seq[s]:
+                    load_w2(e)
             if s == NE:
                 nc.sync.dma_start(pos1_sb[:], pos1)
                 nc.sync.dma_start(pos2_sb[:], pos2)
@@ -120,11 +126,11 @@ def tile_moe_shr_mlp_relu_kernel(tc, xT, w1, w2, gate, offs, pos1, pos2, out):
         xc = {}
 
         def gather(c):
-            xg[c] = grp.tile([P, CHUNK * J], BF16, name="xg", align_bytes=64)
+            xg[c] = grp.tile([P, GCH * J], BF16, name="xg", align_bytes=64)
             words = xg[c][:].bitcast(U32).rearrange("p (s u) -> p s u", u=2)
             for u in range(2):
                 window = x_pair[:, u * 2 * T : (u + 1) * 2 * T].bitcast(U32)
-                lst = offs_sb[:, c * (CHUNK // 16) : (c + 1) * (CHUNK // 16)]
+                lst = offs_sb[:, c * (GCH // 16) : (c + 1) * (GCH // 16)]
                 nc.vector.tensor_copy(out=words[:, :, u], in_=window.indirect(lst))
 
         def quant(src, width, cname, pool):
@@ -134,20 +140,21 @@ def tile_moe_shr_mlp_relu_kernel(tc, xT, w1, w2, gate, offs, pos1, pos2, out):
             return codes, scales
 
         def quant_x(c):
-            xc[c] = quant(xg[c][:], CHUNK, "xq", cod)
+            xc[c] = quant(xg[c][:], GCH, "xq", cod)
 
         x4 = keep.tile([P, T * J], BF16, name="x4", align_bytes=64)
 
         def cast_x4():
             if X4E == "G":
-                nc.gpsimd.tensor_scalar(
-                    out=x4[:].rearrange("p (t j) -> p t j", j=J),
-                    in0=x_raw[:].rearrange("p j t -> p t j"),
-                    scalar1=1.0,
-                    scalar2=0.0,
-                    op0=MULT,
-                    op1=ADD,
-                )
+                for lo, hi in ((0, CHUNK), (CHUNK, T)):
+                    nc.gpsimd.tensor_scalar(
+                        out=x4[:, lo * J : hi * J].rearrange("p (t j) -> p t j", j=J),
+                        in0=x_raw[:, :, lo:hi].rearrange("p j t -> p t j"),
+                        scalar1=1.0,
+                        scalar2=0.0,
+                        op0=MULT,
+                        op1=ADD,
+                    )
                 return
             dst = x4[:].rearrange("p (b i j) -> p b j i", i=4, j=J)
             src = x_raw[:].rearrange("p j (b i) -> p b j i", i=4)
@@ -159,33 +166,33 @@ def tile_moe_shr_mlp_relu_kernel(tc, xT, w1, w2, gate, offs, pos1, pos2, out):
 
         w1_grp, w2_grp, w1_q, w2_q = {}, {}, {}, {}
 
-        def group_w1(e):
-            w1_grp[e] = grp.tile([P, H * J], BF16, name="w1_grp", align_bytes=64)
-            dst = w1_grp[e][:].rearrange("p (t m j) -> p m j t", t=4, j=J)
-            src = w1_raw[e][:].rearrange("p j (m t) -> p m j t", t=4)
-            vm = 0 if e in W1S else VM
-            if vm > 0:
-                nc.vector.tensor_copy(out=dst[:, :vm], in_=src[:, :vm])
-            if vm < P:
-                step = (P - vm) // (W1_PARTS if vm == 0 else 1)
-                for m in range(vm, P, step):
-                    nc.scalar.copy(out=dst[:, m : m + step], in_=src[:, m : m + step])
-
-        def group_w2(e):
-            w2_grp[e] = grp.tile([P, N * J], BF16, name="w2_grp", align_bytes=64)
-            dst = w2_grp[e][:].rearrange("p (b i j) -> p b j i", i=4, j=J)
-            src = w2_raw[e][:].rearrange("p j (b i) -> p b j i", i=4)
-            v = VW2L if e == E - 1 else VW2S if e in W1S else VW2
+        def cut(dst, src, total, v, parts=1):
             if v > 0:
                 nc.vector.tensor_copy(out=dst[:, :v], in_=src[:, :v])
-            if v < N // 4:
+            if v < total:
                 nc.scalar.copy(out=dst[:, v:], in_=src[:, v:])
 
-        def quant_w1(e):
-            w1_q[e] = quant(w1_grp[e][:], H, "w1_q", cod)
+        def group_w1(g):
+            n = len(g)
+            w1_grp[g] = grp1.tile([P, n * H * J], BF16, name="w1_grp", align_bytes=64)
+            for k, e in enumerate(g):
+                dst = w1_grp[g][:, k * H * J : (k + 1) * H * J].rearrange("p (t m j) -> p m j t", t=4, j=J)
+                src = w1_raw[e][:].rearrange("p j (m t) -> p m j t", t=4)
+                cut(dst, src, P, SHV if e == E else VMS if n == 1 else (P, VMB)[k])
 
-        def quant_w2(e):
-            w2_q[e] = quant(w2_grp[e][:], N, "w2_q", cod)
+        def group_w2(g):
+            n = len(g)
+            w2_grp[g] = grp2.tile([P, n * N * J], BF16, name="w2_grp", align_bytes=64)
+            for k, e in enumerate(g):
+                dst = w2_grp[g][:, k * N * J : (k + 1) * N * J].rearrange("p (b i j) -> p b j i", i=4, j=J)
+                src = w2_raw[e][:].rearrange("p j (b i) -> p b j i", i=4)
+                cut(dst, src, N // 4, 0 if e == E else VWS if n == 1 else (0, VWB)[k])
+
+        def quant_w1(g):
+            w1_q[g] = quant(w1_grp[g][:], len(g) * H, "w1_q", cod)
+
+        def quant_w2(g):
+            w2_q[g] = quant(w2_grp[g][:], len(g) * N, "w2_q", cod)
 
         y_slots = [keep.tile([P, S], F32, name=f"y{r}") for r in range(R)]
         h4, hq = {}, {}
@@ -203,10 +210,10 @@ def tile_moe_shr_mlp_relu_kernel(tc, xT, w1, w2, gate, offs, pos1, pos2, out):
                 stop=True,
             )
 
-        def layer1(wq, x, cols, h_dst, on_vector):
+        def layer1(wq, lo, x, cols, h_dst, on_vector):
             a = pa.tile([P, J, C], F32, name="a")
             for t in range(J):
-                mx(a[:, t, :], wq, t * P, x[0][:, cols], x[1][:, cols])
+                mx(a[:, t, :], wq, lo + t * P, x[0][:, cols], x[1][:, cols])
             dst = h_dst.rearrange("p (c t) -> p c t", t=J)
             src = a[:].rearrange("p t c -> p c t")
             if on_vector:
@@ -218,19 +225,20 @@ def tile_moe_shr_mlp_relu_kernel(tc, xT, w1, w2, gate, offs, pos1, pos2, out):
             xs["a"] = quant(x4[:, : CHUNK * J], CHUNK, "xs_a", keep)
             xs["b"] = quant(x4[:, CHUNK * J :], T - CHUNK, "xs_b", keep)
 
-        def op_l1(e):
-            if e < E:
-                h4[e] = hid.tile([P, C * J], BF16, name="h4", align_bytes=64)
-                c, o = divmod(e * C, CHUNK)
-                layer1(w1_q[e], xc[c], slice(o, o + C), h4[e][:], e in RELUV)
+        def op_l1(g):
+            if g == (E,):
+                for c in range(T // C):
+                    x, o = (xs["a"], c * C) if c * C < CHUNK else (xs["b"], c * C - CHUNK)
+                    layer1(w1_q[g], 0, x, slice(o, o + C), hs4[:, c * C * J : (c + 1) * C * J], False)
                 return
-            for c in range(T // C):
-                x, o = (xs["a"], c * C) if c * C < CHUNK else (xs["b"], c * C - CHUNK)
-                layer1(w1_q[E], x, slice(o, o + C), hs4[:, c * C * J : (c + 1) * C * J], False)
+            h4[g] = hid.tile([P, len(g) * C * J], BF16, name="h4", align_bytes=64)
+            for k, e in enumerate(g):
+                c, o = divmod(e * C, GCH)
+                layer1(w1_q[g], k * H, xc[c], slice(o, o + C), h4[g][:, k * C * J : (k + 1) * C * J], e in RELUV)
 
-        def op_qh(e):
-            if e < E:
-                hq[e] = quant(h4[e][:], C, "hq", hid)
+        def op_qh(g):
+            if g != (E,):
+                hq[g] = quant(h4[g][:], len(g) * C, "hq", hid)
                 return
             hs["a"] = quant(hs4[:, : CHUNK * J], CHUNK, "hs_a", keep)
             hs["b"] = quant(hs4[:, CHUNK * J :], T - CHUNK, "hs_b", keep)
@@ -244,25 +252,25 @@ def tile_moe_shr_mlp_relu_kernel(tc, xT, w1, w2, gate, offs, pos1, pos2, out):
             {"a": bank2[:], "b": bank1[:, 1, :]},
         ]
 
-        def op_l2(e):
-            if e == E:
+        def op_l2(g):
+            if g == (E,):
                 for k in "ab":
                     for r in range(R):
-                        mx(ys[r][k], w2_q[E], r * P, hs[k][0][:], hs[k][1][:])
+                        mx(ys[r][k], w2_q[g], r * P, hs[k][0][:], hs[k][1][:])
                 return
-            if e % 2 == 0:
-                y_ps[0] = py.tile([P, R, 2, C], F32, name="y_ps")
-            y = y_ps[0]
-            for r in range(R):
-                mx(y[:, r, e % 2, :], w2_q[e], r * P, hq[e][0][:], hq[e][1][:])
-            if e % 2 == 1:
+            n = len(g)
+            y = py.tile([P, R, n, C], F32, name="y_ps")
+            for k in range(n):
                 for r in range(R):
-                    dst = y_slots[r][:, (e - 1) * C : (e + 1) * C]
-                    src = y[:, r, :, :].rearrange("p e c -> p (e c)")
-                    if (e, r) in YV:
-                        nc.vector.tensor_copy(out=dst, in_=src)
-                    else:
-                        nc.scalar.copy(out=dst, in_=src)
+                    cols = slice(k * C, (k + 1) * C)
+                    mx(y[:, r, k, :], w2_q[g], k * N + r * P, hq[g][0][:, cols], hq[g][1][:, cols])
+            for r in range(R):
+                dst = y_slots[r][:, g[0] * C : (g[0] + n) * C]
+                src = y[:, r, :, :].rearrange("p e c -> p (e c)")
+                if (g[0], r) in YV:
+                    nc.vector.tensor_copy(out=dst, in_=src)
+                else:
+                    nc.scalar.copy(out=dst, in_=src)
 
         steps = {
             "w1": (0, group_w1),
@@ -285,11 +293,11 @@ def tile_moe_shr_mlp_relu_kernel(tc, xT, w1, w2, gate, offs, pos1, pos2, out):
                 cast_x4()
             if s == XSQ_STEP:
                 quant_xs()
-            for c, g in enumerate((G0_STEP, G1_STEP, G2_STEP)):
+            for c in range(S // GCH):
+                g = max(min(q for q in range(NE) if c * GCH // C in seq[q]) + LAG_L1 - GL, 0)
                 if s == g:
                     gather(c)
-            for c, g in enumerate((G0_STEP, G1_STEP + 1, G2_STEP + 1)):
-                if s == g:
+                if s == g + GQ:
                     quant_x(c)
             for op in ORDER:
                 lag, fn = steps[op]

@@ -20,8 +20,8 @@ MULT = mybir.AluOpType.mult
 ADD = mybir.AluOpType.add
 
 CHUNK = 512
-GROUPS = ((0, 1), (2, 3), (4, 5), (6, 7), (8, 9), (10,), (11,))
-AHEAD = 3
+GROUPS = ((0,), (1, 2), (3, 4), (5, 6), (7, 8), (9, 10), (11,))
+AHEAD = 1
 RAW1 = 4
 RAW2 = 3
 GRP1 = 2
@@ -29,29 +29,37 @@ GRP2 = 2
 COD = 3
 XP1 = 'S'
 X4E = 'G'
-SPOS = 0
+SPOS = 1
 SHV = 0
-VMB = 64
-VMS = 80
-VWB = 0
-VWS = 64
+VMB = 32
+VMS = 128
+VWB = 48
+VWS = 0
 LAG_Q1 = 1
 LAG_W2 = 1
-LAG_Q2 = 1
+LAG_Q2 = 2
 LAG_L1 = 1
 LAG_QH = 2
 LAG_L2 = 2
-ORDER = ('q1', 'l1', 'w1', 'w2', 'qh', 'q2', 'l2')
+ORDER = ('q1', 'w1', 'q2', 'qh', 'w2', 'l1', 'l2')
 GCH = 512
 GL = 3
 GQ = 0
-X4_STEP = -1
-XSQ_STEP = 0
+X4_STEP = 1
+XSQ_STEP = 2
 PA = 3
-RELUV = ()
-YV = ()
+RELUV = (11,)
+YV = ((11, 1),)
 HALVES = 1
-YSB = False
+PLAN = False
+ORDER_END = ('q2', 'l1', 'qh', 'w2', 'w1', 'q1', 'l2')
+EOFF = 9
+GRING = 2
+GW1 = (0,)
+GW2 = (12,)
+W1LEAD = True
+XSPLIT = True
+XP0 = 'V'
 
 
 def tile_moe_shr_mlp_relu_kernel(tc, xT, w1, w2, gate, offs, pos1, pos2, out):
@@ -82,7 +90,8 @@ def tile_moe_shr_mlp_relu_kernel(tc, xT, w1, w2, gate, offs, pos1, pos2, out):
         x_raw = keep.tile([P, J, T], F32, name="x_raw")
         x_rows = xT.rearrange("(p j) t -> p j t", j=J)
         for u in range(2):
-            nc.sync.dma_start(out=x_raw[:, 2 * u : 2 * u + 2, :], in_=x_rows[:, 2 * u : 2 * u + 2, :])
+            for lo, hi in ((0, T // 2), (T // 2, T)) if XSPLIT and u == 0 else ((0, T),):
+                nc.sync.dma_start(out=x_raw[:, 2 * u : 2 * u + 2, lo:hi], in_=x_rows[:, 2 * u : 2 * u + 2, lo:hi])
 
         w1_raw, w2_raw = {}, {}
 
@@ -97,11 +106,16 @@ def tile_moe_shr_mlp_relu_kernel(tc, xT, w1, w2, gate, offs, pos1, pos2, out):
         gates = {}
 
         def load_gate(r):
-            gates[r] = raw1.tile([P, 2, T], F32, name="w1_raw")
+            gates[r] = raw1.tile([P, 2, T], F32, name="w1_raw") if GRING == 1 else raw2.tile([P, 2, T], F32, name="w2_raw")
             nc.sync.dma_start(out=gates[r][:], in_=gate[:, r * P : (r + 1) * P, :].rearrange("c p t -> p c t"))
 
         def load_step(s):
-            if s < NE:
+            if W1LEAD:
+                for e in seq[s] if s < NE else ():
+                    load_w1(e)
+                for e in seq[s - 1] if 1 <= s <= NE else ():
+                    load_w2(e)
+            elif s < NE:
                 for e in seq[s]:
                     load_w1(e)
                 for e in seq[s]:
@@ -117,10 +131,11 @@ def tile_moe_shr_mlp_relu_kernel(tc, xT, w1, w2, gate, offs, pos1, pos2, out):
         def cast_pair(u):
             dst = x_pair[:, u * 2 * T : (u + 1) * 2 * T].rearrange("p (b i e) -> p b e i", i=4, e=2)
             src = x_raw[:, 2 * u : 2 * u + 2, :].rearrange("p e (b i) -> p b e i", i=4)
-            if u == 0 or XP1 == "V":
-                nc.vector.tensor_copy(out=dst, in_=src)
-            else:
-                nc.scalar.copy(out=dst, in_=src)
+            for lo, hi in ((0, T // 8), (T // 8, T // 4)) if XSPLIT and u == 0 else ((0, T // 4),):
+                if (XP0, XP1)[u] == "V":
+                    nc.vector.tensor_copy(out=dst[:, lo:hi], in_=src[:, lo:hi])
+                else:
+                    nc.scalar.copy(out=dst[:, lo:hi], in_=src[:, lo:hi])
 
         xg = {}
         xc = {}
@@ -128,10 +143,22 @@ def tile_moe_shr_mlp_relu_kernel(tc, xT, w1, w2, gate, offs, pos1, pos2, out):
         def gather(c):
             xg[c] = grp.tile([P, GCH * J], BF16, name="xg", align_bytes=64)
             words = xg[c][:].bitcast(U32).rearrange("p (s u) -> p s u", u=2)
+            if PLAN:
+                xp = grp.tile([P, 2 * GCH * 2], BF16, name="xp", align_bytes=64)
             for u in range(2):
                 window = x_pair[:, u * 2 * T : (u + 1) * 2 * T].bitcast(U32)
                 lst = offs_sb[:, c * (GCH // 16) : (c + 1) * (GCH // 16)]
-                nc.vector.tensor_copy(out=words[:, :, u], in_=window.indirect(lst))
+                if PLAN:
+                    nc.vector.tensor_copy(
+                        out=xp[:, u * 2 * GCH : (u + 1) * 2 * GCH].bitcast(U32), in_=window.indirect(lst)
+                    )
+                else:
+                    nc.vector.tensor_copy(out=words[:, :, u], in_=window.indirect(lst))
+            if PLAN:
+                nc.scalar.copy(
+                    out=xg[c][:].rearrange("p (s u e) -> p s u e", u=2, e=2),
+                    in_=xp[:].rearrange("p (u s e) -> p s u e", u=2, e=2),
+                )
 
         def quant(src, width, cname, pool):
             codes = pool.tile([P, width], U32, name=cname, align_bytes=64)
@@ -166,7 +193,10 @@ def tile_moe_shr_mlp_relu_kernel(tc, xT, w1, w2, gate, offs, pos1, pos2, out):
 
         w1_grp, w2_grp, w1_q, w2_q = {}, {}, {}, {}
 
-        def cut(dst, src, total, v, parts=1):
+        def cut(dst, src, total, v, on_gpsimd):
+            if on_gpsimd:
+                nc.gpsimd.tensor_scalar(out=dst, in0=src, scalar1=1.0, scalar2=0.0, op0=MULT, op1=ADD)
+                return
             if v > 0:
                 nc.vector.tensor_copy(out=dst[:, :v], in_=src[:, :v])
             if v < total:
@@ -176,17 +206,19 @@ def tile_moe_shr_mlp_relu_kernel(tc, xT, w1, w2, gate, offs, pos1, pos2, out):
             n = len(g)
             w1_grp[g] = grp1.tile([P, n * H * J], BF16, name="w1_grp", align_bytes=64)
             for k, e in enumerate(g):
-                dst = w1_grp[g][:, k * H * J : (k + 1) * H * J].rearrange("p (t m j) -> p m j t", t=4, j=J)
-                src = w1_raw[e][:].rearrange("p j (m t) -> p m j t", t=4)
-                cut(dst, src, P, SHV if e == E else VMS if n == 1 else (P, VMB)[k])
+                order = "t m j" if e in GW1 else "m j t"
+                dst = w1_grp[g][:, k * H * J : (k + 1) * H * J].rearrange("p (t m j) -> p " + order, t=4, j=J)
+                src = w1_raw[e][:].rearrange("p j (m t) -> p " + order, t=4)
+                cut(dst, src, P, SHV if e == E else VMS if n == 1 else (P, VMB)[k], e in GW1)
 
         def group_w2(g):
             n = len(g)
             w2_grp[g] = grp2.tile([P, n * N * J], BF16, name="w2_grp", align_bytes=64)
             for k, e in enumerate(g):
-                dst = w2_grp[g][:, k * N * J : (k + 1) * N * J].rearrange("p (b i j) -> p b j i", i=4, j=J)
-                src = w2_raw[e][:].rearrange("p j (b i) -> p b j i", i=4)
-                cut(dst, src, N // 4, 0 if e == E else VWS if n == 1 else (0, VWB)[k])
+                order = "b i j" if e in GW2 else "b j i"
+                dst = w2_grp[g][:, k * N * J : (k + 1) * N * J].rearrange("p (b i j) -> p " + order, i=4, j=J)
+                src = w2_raw[e][:].rearrange("p j (b i) -> p " + order, i=4)
+                cut(dst, src, N // 4, 0 if e == E else VWS if n == 1 else (0, VWB)[k], e in GW2)
 
         def quant_w1(g):
             w1_q[g] = quant(w1_grp[g][:], len(g) * H, "w1_q", cod)
@@ -299,7 +331,7 @@ def tile_moe_shr_mlp_relu_kernel(tc, xT, w1, w2, gate, offs, pos1, pos2, out):
                     gather(c)
                 if s == g + GQ:
                     quant_x(c)
-            for op in ORDER:
+            for op in ORDER_END if s >= NE - 1 + EOFF else ORDER:
                 lag, fn = steps[op]
                 if 0 <= s - lag < NE:
                     fn(seq[s - lag])

from contextlib import ExitStack

import concourse.mybir as mybir

K, T, E, C, H, N = 512, 768, 12, 128, 512, 256
S = E * C
P = 128
J = 4
R = N // P
FLOPS = 2 * (S + T) * (K * H + H * N)

F32 = mybir.dt.float32
BF16 = mybir.dt.bfloat16
U32 = mybir.dt.uint32
U16 = mybir.dt.uint16
U8 = mybir.dt.uint8
FP8X4 = mybir.dt.float8_e4m3fn_x4
RELU = mybir.ActivationFunctionType.Relu
MULT = mybir.AluOpType.mult
ADD = mybir.AluOpType.add

CHUNK = 512
GROUPS = ((0,), (1, 2), (3, 4), (5, 6), (7, 8), (9, 10), (11,))
AHEAD = 1
RAW1 = 4
RAW2 = 3
GRP1 = 2
GRP2 = 2
COD = 3
XP1 = 'S'
X4E = 'G'
SPOS = 1
SHV = 0
VMB = 32
VMS = 128
VWB = 48
VWS = 0
LAG_Q1 = 1
LAG_W2 = 1
LAG_Q2 = 2
LAG_L1 = 1
LAG_QH = 2
LAG_L2 = 2
ORDER = ('q1', 'w1', 'q2', 'qh', 'w2', 'l1', 'l2')
GCH = 512
GL = 3
GQ = 0
X4_STEP = 1
XSQ_STEP = 2
PA = 3
RELUV = (11,)
YV = ((11, 1),)
HALVES = 1
PLAN = False
ORDER_END = ('q2', 'l1', 'qh', 'w2', 'w1', 'q1', 'l2')
EOFF = 9
GRING = 2
GW1 = (0,)
GW2 = (12,)
W1LEAD = True
XSPLIT = True
XP0 = 'V'


def tile_moe_shr_mlp_relu_kernel(tc, xT, w1, w2, gate, offs, pos1, pos2, out):
    nc = tc.nc
    with ExitStack() as ctx:
        lists = ctx.enter_context(tc.tile_pool(name="lists", bufs=1))
        keep = ctx.enter_context(tc.tile_pool(name="keep", bufs=1))
        raw1 = ctx.enter_context(tc.tile_pool(name="raw1", bufs=RAW1))
        raw2 = ctx.enter_context(tc.tile_pool(name="raw2", bufs=RAW2))
        grp = ctx.enter_context(tc.tile_pool(name="grp", bufs=2))
        grp1 = ctx.enter_context(tc.tile_pool(name="grp1", bufs=GRP1))
        grp2 = ctx.enter_context(tc.tile_pool(name="grp2", bufs=GRP2))
        cod = ctx.enter_context(tc.tile_pool(name="cod", bufs=COD))
        hid = ctx.enter_context(tc.tile_pool(name="hid", bufs=2))
        fin = ctx.enter_context(tc.tile_pool(name="fin", bufs=2))
        pa = ctx.enter_context(tc.psum_pool(name="pa", bufs=PA))
        py = ctx.enter_context(tc.psum_pool(name="py", bufs=2))
        ps = ctx.enter_context(tc.psum_pool(name="ps", bufs=1))

        seq = list(GROUPS)
        seq.insert(SPOS, (E,))
        NE = len(seq)

        offs_sb = lists.tile([P, S // 16], U16, name="offs_sb")
        pos1_sb = lists.tile([P, T // 16], U16, name="pos1_sb")
        pos2_sb = lists.tile([P, T // 16], U16, name="pos2_sb")
        nc.sync.dma_start(offs_sb[:], offs)
        x_raw = keep.tile([P, J, T], F32, name="x_raw")
        x_rows = xT.rearrange("(p j) t -> p j t", j=J)
        for u in range(2):
            for lo, hi in ((0, T // 2), (T // 2, T)) if XSPLIT and u == 0 else ((0, T),):
                nc.sync.dma_start(out=x_raw[:, 2 * u : 2 * u + 2, lo:hi], in_=x_rows[:, 2 * u : 2 * u + 2, lo:hi])

        w1_raw, w2_raw = {}, {}

        def load_w1(e):
            w1_raw[e] = raw1.tile([P, J, H], F32, name="w1_raw")
            nc.sync.dma_start(out=w1_raw[e][:], in_=w1[e].rearrange("(p j) i -> p j i", j=J))

        def load_w2(e):
            w2_raw[e] = raw2.tile([P, J, N], F32, name="w2_raw")
            nc.sync.dma_start(out=w2_raw[e][:], in_=w2[e].rearrange("(p j) n -> p j n", j=J))

        gates = {}

        def load_gate(r):
            gates[r] = raw1.tile([P, 2, T], F32, name="w1_raw") if GRING == 1 else raw2.tile([P, 2, T], F32, name="w2_raw")
            nc.sync.dma_start(out=gates[r][:], in_=gate[:, r * P : (r + 1) * P, :].rearrange("c p t -> p c t"))

        def load_step(s):
            if W1LEAD:
                for e in seq[s] if s < NE else ():
                    load_w1(e)
                for e in seq[s - 1] if 1 <= s <= NE else ():
                    load_w2(e)
            elif s < NE:
                for e in seq[s]:
                    load_w1(e)
                for e in seq[s]:
                    load_w2(e)
            if s == NE:
                nc.sync.dma_start(pos1_sb[:], pos1)
                nc.sync.dma_start(pos2_sb[:], pos2)
                load_gate(0)
                load_gate(1)

        x_pair = keep.tile([P, 2 * T * 2], BF16, name="x_pair", align_bytes=64)

        def cast_pair(u):
            dst = x_pair[:, u * 2 * T : (u + 1) * 2 * T].rearrange("p (b i e) -> p b e i", i=4, e=2)
            src = x_raw[:, 2 * u : 2 * u + 2, :].rearrange("p e (b i) -> p b e i", i=4)
            for lo, hi in ((0, T // 8), (T // 8, T // 4)) if XSPLIT and u == 0 else ((0, T // 4),):
                if (XP0, XP1)[u] == "V":
                    nc.vector.tensor_copy(out=dst[:, lo:hi], in_=src[:, lo:hi])
                else:
                    nc.scalar.copy(out=dst[:, lo:hi], in_=src[:, lo:hi])

        xg = {}
        xc = {}

        def gather(c):
            xg[c] = grp.tile([P, GCH * J], BF16, name="xg", align_bytes=64)
            words = xg[c][:].bitcast(U32).rearrange("p (s u) -> p s u", u=2)
            if PLAN:
                xp = grp.tile([P, 2 * GCH * 2], BF16, name="xp", align_bytes=64)
            for u in range(2):
                window = x_pair[:, u * 2 * T : (u + 1) * 2 * T].bitcast(U32)
                lst = offs_sb[:, c * (GCH // 16) : (c + 1) * (GCH // 16)]
                if PLAN:
                    nc.vector.tensor_copy(
                        out=xp[:, u * 2 * GCH : (u + 1) * 2 * GCH].bitcast(U32), in_=window.indirect(lst)
                    )
                else:
                    nc.vector.tensor_copy(out=words[:, :, u], in_=window.indirect(lst))
            if PLAN:
                nc.scalar.copy(
                    out=xg[c][:].rearrange("p (s u e) -> p s u e", u=2, e=2),
                    in_=xp[:].rearrange("p (u s e) -> p s u e", u=2, e=2),
                )

        def quant(src, width, cname, pool):
            codes = pool.tile([P, width], U32, name=cname, align_bytes=64)
            scales = pool.tile([P, width], U8, name=cname + "_sc", align_bytes=64)
            nc.vector.quantize_mx(out=codes[:].bitcast(FP8X4), scales=scales[:], in_=src)
            return codes, scales

        def quant_x(c):
            xc[c] = quant(xg[c][:], GCH, "xq", cod)

        x4 = keep.tile([P, T * J], BF16, name="x4", align_bytes=64)

        def cast_x4():
            if X4E == "G":
                for lo, hi in ((0, CHUNK), (CHUNK, T)):
                    nc.gpsimd.tensor_scalar(
                        out=x4[:, lo * J : hi * J].rearrange("p (t j) -> p t j", j=J),
                        in0=x_raw[:, :, lo:hi].rearrange("p j t -> p t j"),
                        scalar1=1.0,
                        scalar2=0.0,
                        op0=MULT,
                        op1=ADD,
                    )
                return
            dst = x4[:].rearrange("p (b i j) -> p b j i", i=4, j=J)
            src = x_raw[:].rearrange("p j (b i) -> p b j i", i=4)
            for lo, hi in ((0, CHUNK // 4), (CHUNK // 4, T // 4)):
                if X4E == "S":
                    nc.scalar.copy(out=dst[:, lo:hi], in_=src[:, lo:hi])
                else:
                    nc.vector.tensor_copy(out=dst[:, lo:hi], in_=src[:, lo:hi])

        w1_grp, w2_grp, w1_q, w2_q = {}, {}, {}, {}

        def cut(dst, src, total, v, on_gpsimd):
            if on_gpsimd:
                nc.gpsimd.tensor_scalar(out=dst, in0=src, scalar1=1.0, scalar2=0.0, op0=MULT, op1=ADD)
                return
            if v > 0:
                nc.vector.tensor_copy(out=dst[:, :v], in_=src[:, :v])
            if v < total:
                nc.scalar.copy(out=dst[:, v:], in_=src[:, v:])

        def group_w1(g):
            n = len(g)
            w1_grp[g] = grp1.tile([P, n * H * J], BF16, name="w1_grp", align_bytes=64)
            for k, e in enumerate(g):
                order = "t m j" if e in GW1 else "m j t"
                dst = w1_grp[g][:, k * H * J : (k + 1) * H * J].rearrange("p (t m j) -> p " + order, t=4, j=J)
                src = w1_raw[e][:].rearrange("p j (m t) -> p " + order, t=4)
                cut(dst, src, P, SHV if e == E else VMS if n == 1 else (P, VMB)[k], e in GW1)

        def group_w2(g):
            n = len(g)
            w2_grp[g] = grp2.tile([P, n * N * J], BF16, name="w2_grp", align_bytes=64)
            for k, e in enumerate(g):
                order = "b i j" if e in GW2 else "b j i"
                dst = w2_grp[g][:, k * N * J : (k + 1) * N * J].rearrange("p (b i j) -> p " + order, i=4, j=J)
                src = w2_raw[e][:].rearrange("p j (b i) -> p " + order, i=4)
                cut(dst, src, N // 4, 0 if e == E else VWS if n == 1 else (0, VWB)[k], e in GW2)

        def quant_w1(g):
            w1_q[g] = quant(w1_grp[g][:], len(g) * H, "w1_q", cod)

        def quant_w2(g):
            w2_q[g] = quant(w2_grp[g][:], len(g) * N, "w2_q", cod)

        y_slots = [keep.tile([P, S], F32, name=f"y{r}") for r in range(R)]
        h4, hq = {}, {}
        hs4 = keep.tile([P, T * J], BF16, name="hs4", align_bytes=64)
        xs, hs = {}, {}

        def mx(dst, w, lo, xcodes, xscales):
            nc.tensor.matmul_mx(
                out=dst,
                lhsT=w[0][:, lo : lo + P].bitcast(FP8X4),
                lhsT_scale=w[1][:, lo : lo + P],
                rhs=xcodes.bitcast(FP8X4),
                rhs_scale=xscales,
                start=True,
                stop=True,
            )

        def layer1(wq, lo, x, cols, h_dst, on_vector):
            a = pa.tile([P, J, C], F32, name="a")
            for t in range(J):
                mx(a[:, t, :], wq, lo + t * P, x[0][:, cols], x[1][:, cols])
            dst = h_dst.rearrange("p (c t) -> p c t", t=J)
            src = a[:].rearrange("p t c -> p c t")
            if on_vector:
                nc.vector.tensor_scalar_max(dst, src, 0.0)
            else:
                nc.scalar.activation(out=dst, in_=src, func=RELU)

        def quant_xs():
            xs["a"] = quant(x4[:, : CHUNK * J], CHUNK, "xs_a", keep)
            xs["b"] = quant(x4[:, CHUNK * J :], T - CHUNK, "xs_b", keep)

        def op_l1(g):
            if g == (E,):
                for c in range(T // C):
                    x, o = (xs["a"], c * C) if c * C < CHUNK else (xs["b"], c * C - CHUNK)
                    layer1(w1_q[g], 0, x, slice(o, o + C), hs4[:, c * C * J : (c + 1) * C * J], False)
                return
            h4[g] = hid.tile([P, len(g) * C * J], BF16, name="h4", align_bytes=64)
            for k, e in enumerate(g):
                c, o = divmod(e * C, GCH)
                layer1(w1_q[g], k * H, xc[c], slice(o, o + C), h4[g][:, k * C * J : (k + 1) * C * J], e in RELUV)

        def op_qh(g):
            if g != (E,):
                hq[g] = quant(h4[g][:], len(g) * C, "hq", hid)
                return
            hs["a"] = quant(hs4[:, : CHUNK * J], CHUNK, "hs_a", keep)
            hs["b"] = quant(hs4[:, CHUNK * J :], T - CHUNK, "hs_b", keep)

        y_ps = {}
        bank0 = ps.tile([P, CHUNK], F32, name="bank0")
        bank1 = ps.tile([P, 2, T - CHUNK], F32, name="bank1")
        bank2 = ps.tile([P, CHUNK], F32, name="bank2")
        ys = [
            {"a": bank0[:], "b": bank1[:, 0, :]},
            {"a": bank2[:], "b": bank1[:, 1, :]},
        ]

        def op_l2(g):
            if g == (E,):
                for k in "ab":
                    for r in range(R):
                        mx(ys[r][k], w2_q[g], r * P, hs[k][0][:], hs[k][1][:])
                return
            n = len(g)
            y = py.tile([P, R, n, C], F32, name="y_ps")
            for k in range(n):
                for r in range(R):
                    cols = slice(k * C, (k + 1) * C)
                    mx(y[:, r, k, :], w2_q[g], k * N + r * P, hq[g][0][:, cols], hq[g][1][:, cols])
            for r in range(R):
                dst = y_slots[r][:, g[0] * C : (g[0] + n) * C]
                src = y[:, r, :, :].rearrange("p e c -> p (e c)")
                if (g[0], r) in YV:
                    nc.vector.tensor_copy(out=dst, in_=src)
                else:
                    nc.scalar.copy(out=dst, in_=src)

        steps = {
            "w1": (0, group_w1),
            "w2": (LAG_W2, group_w2),
            "q1": (LAG_Q1, quant_w1),
            "q2": (LAG_Q2, quant_w2),
            "l1": (LAG_L1, op_l1),
            "qh": (LAG_QH, op_qh),
            "l2": (LAG_L2, op_l2),
        }
        for s in range(AHEAD):
            load_step(s)
        cast_pair(0)
        cast_pair(1)
        if X4_STEP < 0:
            cast_x4()
        for s in range(NE + max(LAG_L2, LAG_QH) + 1):
            load_step(s + AHEAD)
            if s == X4_STEP:
                cast_x4()
            if s == XSQ_STEP:
                quant_xs()
            for c in range(S // GCH):
                g = max(min(q for q in range(NE) if c * GCH // C in seq[q]) + LAG_L1 - GL, 0)
                if s == g:
                    gather(c)
                if s == g + GQ:
                    quant_x(c)
            for op in ORDER_END if s >= NE - 1 + EOFF else ORDER:
                lag, fn = steps[op]
                if 0 <= s - lag < NE:
                    fn(seq[s - lag])

        w = T // HALVES
        for r in range(R):
            for h in range(HALVES if r == R - 1 else 1):
                tok = slice(h * w, (h + 1) * w) if r == R - 1 else slice(0, T)
                n = tok.stop - tok.start
                g0 = fin.tile([P, T], F32, name="g0")
                g1 = fin.tile([P, T], F32, name="g1")
                both = fin.tile([P, T], F32, name="both")
                for c, (g, lst) in enumerate(((g0, pos1_sb), (g1, pos2_sb))):
                    nc.vector.tensor_tensor(
                        out=g[:, :n],
                        in0=y_slots[r][:].indirect(lst[:, tok.start // 16 : tok.stop // 16]),
                        in1=gates[r][:, c, tok],
                        op=MULT,
                    )
                nc.vector.tensor_tensor(out=both[:, :n], in0=g0[:, :n], in1=g1[:, :n], op=ADD)
                for k, lo, hi in (("a", 0, CHUNK), ("b", CHUNK, T)):
                    a, b = max(lo, tok.start), min(hi, tok.stop)
                    if a < b:
                        res = fin.tile([P, b - a], F32, name=f"res{r}{a}")
                        nc.vector.tensor_tensor(
                            out=res[:], in0=ys[r][k][:, a - lo : b - lo], in1=both[:, a - tok.start : b - tok.start], op=ADD
                        )
                        nc.sync.dma_start(out=out[r * P : (r + 1) * P, a:b], in_=res[:])
